import numpy as np
import ml_dtypes


def mxq(x, axis, fmt="e4m3"):
    dtype, down = {"e4m3": (ml_dtypes.float8_e4m3fn, 7), "e5m2": (ml_dtypes.float8_e5m2, 14)}[fmt]
    v = np.moveaxis(np.asarray(x, np.float32).astype(ml_dtypes.bfloat16).astype(np.float64), axis, -1)
    blocks = v.reshape(v.shape[:-1] + (-1, 32))
    amax = np.abs(blocks).max(-1, keepdims=True)
    byte = np.maximum(np.where(amax > 0, np.frexp(amax)[1] - 1 + 127, 0) - down, 1)
    scale = np.exp2(byte - 127.0)
    codes = (blocks / scale).astype(np.float32).astype(dtype).astype(np.float64)
    return np.moveaxis((codes * scale).reshape(v.shape), -1, axis)


WIDE = False


def mx_kscale(k):
    if not WIDE:
        return np.ones(k)
    levels = np.array([10, -10, 5, -5, 0])
    if k % 512:
        return np.exp2(np.random.permutation(np.resize(levels, k // 32))).repeat(32)
    a = np.empty((k // 512, 16))
    for p in range(k // 512):
        a[p, :8] = np.random.permutation(np.resize(levels, 8))
        for g in range(8):
            far = levels[np.abs(levels - a[p, g]) >= 10]
            a[p, g + 8] = far[np.random.randint(len(far))]
    return np.exp2(a.ravel()).repeat(32)


def f64(x):
    return np.asarray(x).astype(np.float64)


def striped(idx):
    return np.tile(np.asarray(idx).reshape(-1, 16).T, (8, 1)).astype(np.uint16)


def unstriped(offs):
    return offs[:16].T.reshape(-1).astype(np.int64)


E2M1 = np.array([0.0, 0.5, 1.0, 1.5, 2.0, 3.0, 4.0, 6.0, -0.0, -0.5, -1.0, -1.5, -2.0, -3.0, -4.0, -6.0])


def pack_weight(w, fmt):
    k, n = w.shape
    w = f64(np.asarray(w, np.float32).astype(ml_dtypes.bfloat16)).reshape(k // 32, 32, n)
    amax = np.abs(w).max(1)
    if fmt == "e4m3":
        byte = np.frexp(amax)[1] - 1 + 127 - 7
    else:
        mant, ex = np.frexp(amax / 6.0)
        byte = np.where(mant > 0.5, ex, ex - 1) + 127
    byte = np.clip(np.where(amax > 0, byte, 1), 1, 254)
    scaled = (w * np.exp2(127.0 - byte)[:, None, :]).reshape(k, n).astype(np.float32)
    by_word = np.ascontiguousarray(scaled.reshape(k // 512, 128, 4, n).transpose(0, 1, 3, 2))
    if fmt == "e4m3":
        words = by_word.astype(ml_dtypes.float8_e4m3fn).view(np.uint8)
    else:
        c = by_word.astype(ml_dtypes.float4_e2m1fn).view(np.uint8) & 0xF
        words = (c[..., 0::2] | (c[..., 1::2] << 4)).reshape(k // 512, 128, 2 * n)
    return np.ascontiguousarray(words), np.ascontiguousarray(byte.astype(np.uint8).reshape(k // 512, 16, n))


def unpack_weight(words, scales, fmt):
    g, _, n = scales.shape
    words = np.ascontiguousarray(words).reshape(g, 128, n, -1)
    if fmt == "e4m3":
        vals = words.view(ml_dtypes.float8_e4m3fn).astype(np.float64)
    else:
        nib = np.empty((g, 128, n, 4), np.uint8)
        nib[..., 0::2] = words & 0xF
        nib[..., 1::2] = words >> 4
        vals = E2M1[nib]
    vals = vals * np.repeat(np.exp2(scales.astype(np.float64) - 127.0), 8, axis=1)[..., None]
    return vals.transpose(0, 1, 3, 2).reshape(g * 512, n)


def bf(x):
    return np.asarray(x, np.float32).astype(ml_dtypes.bfloat16)


def planes(Y):
    r, m = Y.shape
    b = f64(bf(Y)).reshape(r // 32, 32, m)
    amax = np.abs(b).max(1)
    byte = np.clip(np.where(amax > 0, np.frexp(amax)[1] - 1 + 127 - 7, 1), 1, 254)
    codes = (b * np.exp2(127.0 - byte)[:, None, :]).reshape(r, m).astype(np.float32).astype(ml_dtypes.float8_e4m3fn).view(np.uint8)
    words = codes.reshape(r // 512, 128, 4, m).transpose(0, 1, 3, 2)
    return np.ascontiguousarray(words), np.ascontiguousarray(byte.astype(np.uint8).reshape(r // 512, 16, m))


K, T, J, L, N, B, S = 512, 2048, 512, 512, 512, 64, 512


def setup_inputs():
    n = np.random.standard_normal
    idx = np.random.permutation(T)[:J]
    idx2 = np.random.permutation(S)[:B]
    fk = mx_kscale(K)
    fl = mx_kscale(L)
    wp = pack_weight(n((K, N)) * 1 / np.sqrt(K) * fk[:, None], "e4m3")
    sxp = pack_weight(n((L, J)) / fl[:, None], "e2m1")
    wsp = pack_weight(n((L, N)) * 1 / np.sqrt(L) * fl[:, None], "e4m3")
    return {
        "xf": (n((K, T))).astype(np.float32),
        "gv": (n((K, S))).astype(np.float32),
        "fk": (np.random.uniform(0.5, 2.0, (K, 1)) / fk[:, None]).astype(np.float32),
        "w_words": wp[0],
        "w_scales": wp[1],
        "sx_words": sxp[0],
        "sx_scales": sxp[1],
        "ws_words": wsp[0],
        "ws_scales": wsp[1],
        "offs": striped(idx),
        "offs2": striped(idx2),
    }


def reference(xf, gv, fk, w_words, w_scales, sx_words, sx_scales, ws_words, ws_scales, offs, offs2):
    idx = unstriped(offs)
    idx2 = unstriped(offs2)
    wu = unpack_weight(w_words, w_scales, "e4m3")
    sxu = unpack_weight(sx_words, sx_scales, "e2m1")
    wsu = unpack_weight(ws_words, ws_scales, "e4m3")
    g1 = f64(gv)[:, idx2]
    gr1 = np.repeat(g1, J // B, axis=1)
    xs = (f64(xf)[:, idx] + gr1) * f64(fk)
    xsq = mxq(xs, 0, "e4m3")
    y = wu.T @ xsq + wsu.T @ sxu
    words, scales = planes(y)
    return y, words, scales

@@ -1,0 +1,185 @@
+from contextlib import ExitStack
+
+import concourse.mybir as mybir
+
+K, T, J, L, N, B, S = 512, 2048, 512, 512, 512, 64, 512
+FLOPS = 2 * K * N * J + 2 * L * N * J
+
+F32 = mybir.dt.float32
+BF16 = mybir.dt.bfloat16
+I32 = mybir.dt.int32
+U16 = mybir.dt.uint16
+U8 = mybir.dt.uint8
+FP8X4 = mybir.dt.float8_e4m3fn_x4
+FP4X4 = mybir.dt.float4_e2m1fn_x4
+ADD = mybir.AluOpType.add
+COPY = mybir.ActivationFunctionType.Copy
+
+P = 128
+PACK = 4
+GROUP = J // B
+PIECE = 128
+PIECES = J // PIECE
+
+
+def load_scale_rows(queue, plane, scales):
+    for quad in range(4):
+        queue.dma_start(
+            out=plane[32 * quad : 32 * quad + 4, :].bitcast(I32),
+            in_=scales[0, 4 * quad : 4 * quad + 4, :].bitcast(I32),
+        )
+
+
+def tile_list_member_plus_picked_group_pl_kernel(
+    tc, xf, gv, fk, w_words, w_scales, sx_words, sx_scales, ws_words, ws_scales, offs, offs2, out_0, out_1, out_2
+):
+    nc = tc.nc
+    with ExitStack() as ctx:
+        sb = ctx.enter_context(tc.tile_pool(name="sb", bufs=1))
+        psum = ctx.enter_context(tc.psum_pool(name="psum", bufs=1))
+
+        slot_list = sb.tile([P, J // 16], U16, name="slot_list")
+        group_list = sb.tile([P, B // 16], U16, name="group_list")
+        gv_sb = sb.tile([P, PACK * S], F32, name="gv_sb")
+        fk_sb = sb.tile([P, PACK], F32, name="fk_sb")
+        xf_sb = [sb.tile([P, T], F32, name="xf_sb%d" % t) for t in range(PACK)]
+        w_raw = sb.tile([P, N], I32, name="w_raw")
+        ws_raw = sb.tile([P, N], I32, name="ws_raw")
+        w_scale_raw = sb.tile([P, N], U8, name="w_scale_raw")
+        ws_scale_raw = sb.tile([P, N], U8, name="ws_scale_raw")
+        sx_codes = sb.tile([P, 2 * J], U8, name="sx_codes", align_bytes=64)
+        sx_scale = sb.tile([P, J], U8, name="sx_scale", align_bytes=64)
+
+        for plane in (ws_scale_raw, w_scale_raw, sx_scale):
+            nc.gpsimd.memset(plane[:].bitcast(I32), 0)
+
+        xf_planes = xf.rearrange("(p t) c -> p t c", t=PACK)
+        nc.sync.dma_start(out=gv_sb[:], in_=gv.rearrange("(p t) s -> p (t s)", t=PACK))
+        nc.sync.dma_start(group_list[:], offs2)
+        nc.sync.dma_start(slot_list[:], offs)
+        nc.sync.dma_start(out=xf_sb[0][:], in_=xf_planes[:, 0, :])
+        nc.scalar.dma_start(out=fk_sb[:], in_=fk.rearrange("(p t) o -> p (t o)", t=PACK))
+        nc.sync.dma_start(out=ws_raw[:], in_=ws_words[0].rearrange("p n t -> p (n t)").bitcast(I32))
+        nc.sync.dma_start(out=w_raw[:], in_=w_words[0].rearrange("p n t -> p (n t)").bitcast(I32))
+        nc.sync.dma_start(out=xf_sb[1][:], in_=xf_planes[:, 1, :])
+        nc.sync.dma_start(out=xf_sb[2][:], in_=xf_planes[:, 2, :])
+        nc.sync.dma_start(out=sx_codes[:].bitcast(I32), in_=sx_words[0].bitcast(I32))
+        nc.sync.dma_start(out=xf_sb[3][:], in_=xf_planes[:, 3, :])
+        load_scale_rows(nc.gpsimd, ws_scale_raw, ws_scales)
+        load_scale_rows(nc.gpsimd, w_scale_raw, w_scales)
+        load_scale_rows(nc.scalar, sx_scale, sx_scales)
+
+        picked = sb.tile([P, PACK, B], F32, name="picked")
+        spread = [sb.tile([P, J], F32, name="spread%d" % t) for t in range(PACK)]
+        for t in range(PACK):
+            nc.vector.tensor_copy(picked[:, t, :], gv_sb[:, t * S : (t + 1) * S].indirect(group_list[:]))
+        for t in range(PACK):
+            nc.vector.tensor_copy(
+                spread[t][:].rearrange("p (b e) -> p b e", e=GROUP),
+                picked[:, t, :].unsqueeze(2).to_broadcast([P, B, GROUP]),
+            )
+
+        xs = [sb.tile([P, PIECE * PACK], BF16, name="xs%d" % q, align_bytes=64) for q in range(PIECES)]
+        summed = [sb.tile([P, J], F32, name="summed%d" % t) for t in range(PACK)]
+
+        def scale_into(t, q):
+            nc.scalar.activation(
+                out=xs[q][:].rearrange("p (j t) -> p j t", t=PACK)[:, :, t],
+                in_=summed[t][:, q * PIECE : (q + 1) * PIECE],
+                func=COPY,
+                scale=fk_sb[:, t : t + 1],
+            )
+
+        def deal(dst, src, run):
+            nc.vector.tensor_copy(
+                dst[:].rearrange("p (t c i) -> p c t i", t=PACK, i=run),
+                src[:].rearrange("p (c i t) -> p c t i", t=PACK, i=run),
+            )
+
+        w_codes = sb.tile([P, N], I32, name="w_codes", align_bytes=64)
+        ws_codes = sb.tile([P, N], I32, name="ws_codes", align_bytes=64)
+        w_scale = sb.tile([P, N], U8, name="w_scale", align_bytes=64)
+        ws_scale = sb.tile([P, N], U8, name="ws_scale", align_bytes=64)
+
+        for t in range(PACK - 1):
+            nc.vector.tensor_tensor(summed[t][:], xf_sb[t][:].indirect(slot_list[:]), spread[t][:], ADD)
+            for q in range(PIECES):
+                scale_into(t, q)
+            if t == 0:
+                deal(ws_codes, ws_raw, 4)
+                deal(w_codes, w_raw, 4)
+            if t == 1:
+                deal(ws_scale, ws_scale_raw, 16)
+                deal(w_scale, w_scale_raw, 16)
+
+        acc = [psum.tile([P, PACK, PIECE], F32, name="acc%d" % q) for q in range(PIECES)]
+        for q in range(PIECES):
+            for t in range(PACK):
+                nc.tensor.matmul_mx(
+                    out=acc[q][:, t, :],
+                    lhsT=ws_codes[:, t * P : (t + 1) * P].bitcast(FP8X4),
+                    lhsT_scale=ws_scale[:, t * P : (t + 1) * P],
+                    rhs=sx_codes[:, 2 * q * PIECE : 2 * (q + 1) * PIECE].bitcast(FP4X4),
+                    rhs_scale=sx_scale[:, q * PIECE : (q + 1) * PIECE],
+                    start=(t == 0),
+                    stop=False,
+                )
+
+        xs_codes = [sb.tile([P, PIECE], I32, name="xs_codes%d" % q, align_bytes=64) for q in range(PIECES)]
+        xs_scale = [sb.tile([P, PIECE], U8, name="xs_scale%d" % q, align_bytes=64) for q in range(PIECES)]
+        y = [sb.tile([P, PACK, PIECE], F32, name="y%d" % q) for q in range(PIECES)]
+        y_round = [sb.tile([P, PIECE * PACK], BF16, name="y_round%d" % q, align_bytes=64) for q in range(PIECES)]
+        y_codes = sb.tile([P, J], I32, name="y_codes", align_bytes=64)
+        y_scale = sb.tile([P, J], U8, name="y_scale", align_bytes=64)
+        out_rows = out_0.rearrange("(p t) j -> p t j", t=PACK)
+        out_words = out_1[0].rearrange("p c t -> p (c t)").bitcast(I32)
+        last = PACK - 1
+
+        def gather_last(q):
+            cols = slice(q * PIECE, (q + 1) * PIECE)
+            entries = slot_list[:, q * PIECE // 16 : (q + 1) * PIECE // 16]
+            nc.vector.tensor_tensor(summed[last][:, cols], xf_sb[last][:].indirect(entries), spread[last][:, cols], ADD)
+            scale_into(last, q)
+
+        def multiply(q):
+            nc.vector.quantize_mx(out=xs_codes[q][:].bitcast(FP8X4), scales=xs_scale[q][:], in_=xs[q][:])
+            for t in range(PACK):
+                nc.tensor.matmul_mx(
+                    out=acc[q][:, t, :],
+                    lhsT=w_codes[:, t * P : (t + 1) * P].bitcast(FP8X4),
+                    lhsT_scale=w_scale[:, t * P : (t + 1) * P],
+                    rhs=xs_codes[q][:].bitcast(FP8X4),
+                    rhs_scale=xs_scale[q][:],
+                    start=False,
+                    stop=(t == PACK - 1),
+                )
+
+        def drain(q):
+            cols = slice(q * PIECE, (q + 1) * PIECE)
+            nc.scalar.copy(out=y[q][:], in_=acc[q][:])
+            nc.sync.dma_start(out=out_rows[:, :, cols], in_=y[q][:])
+
+        def round_y(q):
+            nc.vector.tensor_copy(
+                y_round[q][:].rearrange("p (c i t) -> p c t i", t=PACK, i=4),
+                y[q][:].rearrange("p t (c i) -> p c t i", i=4),
+            )
+
+        def hand_on(q):
+            cols = slice(q * PIECE, (q + 1) * PIECE)
+            nc.vector.quantize_mx(out=y_codes[:, cols].bitcast(FP8X4), scales=y_scale[:, cols], in_=y_round[q][:])
+            if q % 2 == 1:
+                both = slice((q - 1) * PIECE, (q + 1) * PIECE)
+                nc.sync.dma_start(out=out_words[:, both], in_=y_codes[:, both])
+
+        for step in range(PIECES + 4):
+            for lag, stage in ((0, gather_last), (1, multiply), (2, drain), (3, round_y), (4, hand_on)):
+                if 0 <= step - lag < PIECES:
+                    stage(step - lag)
+
+        for quad in range(4):
+            queue = nc.sync if quad % 2 == 0 else nc.scalar
+            queue.dma_start(
+                out=out_2[0, 4 * quad : 4 * quad + 4, :].bitcast(I32),
+                in_=y_scale[32 * quad : 32 * quad + 4, :].bitcast(I32),
+            )

@@ -13,6 +13,7 @@ U8 = mybir.dt.uint8
 FP8X4 = mybir.dt.float8_e4m3fn_x4
 FP4X4 = mybir.dt.float4_e2m1fn_x4
 ADD = mybir.AluOpType.add
+MULT = mybir.AluOpType.mult
 COPY = mybir.ActivationFunctionType.Copy
 
 P = 128
@@ -22,8 +23,8 @@ PIECE = 128
 PIECES = J // PIECE
 
 
-def load_scale_rows(queue, plane, scales):
-    for quad in range(4):
+def load_scale_rows(queue, plane, scales, quads):
+    for quad in quads:
         queue.dma_start(
             out=plane[32 * quad : 32 * quad + 4, :].bitcast(I32),
             in_=scales[0, 4 * quad : 4 * quad + 4, :].bitcast(I32),
@@ -51,23 +52,24 @@ def tile_list_member_plus_picked_group_pl_kernel(
         sx_scale = sb.tile([P, J], U8, name="sx_scale", align_bytes=64)
 
         for plane in (ws_scale_raw, w_scale_raw, sx_scale):
-            nc.gpsimd.memset(plane[:].bitcast(I32), 0)
+            nc.vector.memset(plane[:].bitcast(I32), 0)
 
         xf_planes = xf.rearrange("(p t) c -> p t c", t=PACK)
         nc.sync.dma_start(out=gv_sb[:], in_=gv.rearrange("(p t) s -> p (t s)", t=PACK))
         nc.sync.dma_start(group_list[:], offs2)
         nc.sync.dma_start(slot_list[:], offs)
+        nc.sync.dma_start(out=fk_sb[:], in_=fk.rearrange("(p t) o -> p (t o)", t=PACK))
         nc.sync.dma_start(out=xf_sb[0][:], in_=xf_planes[:, 0, :])
-        nc.scalar.dma_start(out=fk_sb[:], in_=fk.rearrange("(p t) o -> p (t o)", t=PACK))
-        nc.sync.dma_start(out=ws_raw[:], in_=ws_words[0].rearrange("p n t -> p (n t)").bitcast(I32))
-        nc.sync.dma_start(out=w_raw[:], in_=w_words[0].rearrange("p n t -> p (n t)").bitcast(I32))
+        load_scale_rows(nc.sync, ws_scale_raw, ws_scales, range(4))
+        load_scale_rows(nc.sync, w_scale_raw, w_scales, range(2))
         nc.sync.dma_start(out=xf_sb[1][:], in_=xf_planes[:, 1, :])
+        load_scale_rows(nc.sync, w_scale_raw, w_scales, range(2, 4))
+        load_scale_rows(nc.sync, sx_scale, sx_scales, range(4))
         nc.sync.dma_start(out=xf_sb[2][:], in_=xf_planes[:, 2, :])
+        nc.sync.dma_start(out=ws_raw[:], in_=ws_words[0].rearrange("p n t -> p (n t)").bitcast(I32))
         nc.sync.dma_start(out=sx_codes[:].bitcast(I32), in_=sx_words[0].bitcast(I32))
+        nc.sync.dma_start(out=w_raw[:], in_=w_words[0].rearrange("p n t -> p (n t)").bitcast(I32))
         nc.sync.dma_start(out=xf_sb[3][:], in_=xf_planes[:, 3, :])
-        load_scale_rows(nc.gpsimd, ws_scale_raw, ws_scales)
-        load_scale_rows(nc.gpsimd, w_scale_raw, w_scales)
-        load_scale_rows(nc.scalar, sx_scale, sx_scales)
 
         picked = sb.tile([P, PACK, B], F32, name="picked")
         spread = [sb.tile([P, J], F32, name="spread%d" % t) for t in range(PACK)]
@@ -79,16 +81,15 @@ def tile_list_member_plus_picked_group_pl_kernel(
                 picked[:, t, :].unsqueeze(2).to_broadcast([P, B, GROUP]),
             )
 
-        xs = [sb.tile([P, PIECE * PACK], BF16, name="xs%d" % q, align_bytes=64) for q in range(PIECES)]
-        summed = [sb.tile([P, J], F32, name="summed%d" % t) for t in range(PACK)]
+        xs = [sb.tile([P, PIECE * PACK], BF16, name="xs%d" % q, tag="xs%d" % q, align_bytes=64) for q in range(PIECES)]
+        summed = [sb.tile([P, J], F32, name="summed%d" % t) for t in range(PACK - 1)]
 
-        def scale_into(t, q):
-            nc.scalar.activation(
-                out=xs[q][:].rearrange("p (j t) -> p j t", t=PACK)[:, :, t],
-                in_=summed[t][:, q * PIECE : (q + 1) * PIECE],
-                func=COPY,
-                scale=fk_sb[:, t : t + 1],
-            )
+        def scale_into(t, q, src):
+            dst = xs[q][:].rearrange("p (j t) -> p j t", t=PACK)[:, :, t]
+            if q == PIECES - 1 and t >= 2:
+                nc.vector.tensor_scalar(dst, src, fk_sb[:, t : t + 1], None, MULT)
+            else:
+                nc.scalar.activation(out=dst, in_=src, func=COPY, scale=fk_sb[:, t : t + 1])
 
         def deal(dst, src, run):
             nc.vector.tensor_copy(
@@ -104,13 +105,14 @@ def tile_list_member_plus_picked_group_pl_kernel(
         for t in range(PACK - 1):
             nc.vector.tensor_tensor(summed[t][:], xf_sb[t][:].indirect(slot_list[:]), spread[t][:], ADD)
             for q in range(PIECES):
-                scale_into(t, q)
+                scale_into(t, q, summed[t][:, q * PIECE : (q + 1) * PIECE])
             if t == 0:
+                deal(ws_scale, ws_scale_raw, 16)
+            if t == 1:
+                deal(w_scale, w_scale_raw, 16)
+            if t == 2:
                 deal(ws_codes, ws_raw, 4)
                 deal(w_codes, w_raw, 4)
-            if t == 1:
-                deal(ws_scale, ws_scale_raw, 16)
-                deal(w_scale, w_scale_raw, 16)
 
         acc = [psum.tile([P, PACK, PIECE], F32, name="acc%d" % q) for q in range(PIECES)]
         for q in range(PIECES):
@@ -138,8 +140,10 @@ def tile_list_member_plus_picked_group_pl_kernel(
         def gather_last(q):
             cols = slice(q * PIECE, (q + 1) * PIECE)
             entries = slot_list[:, q * PIECE // 16 : (q + 1) * PIECE // 16]
-            nc.vector.tensor_tensor(summed[last][:, cols], xf_sb[last][:].indirect(entries), spread[last][:, cols], ADD)
-            scale_into(last, q)
+            tag = "xs0" if q == PIECES - 1 else "tail%d" % q
+            tail = sb.tile([P, PIECE], F32, name="tail%d" % q, tag=tag, align_bytes=64)
+            nc.vector.tensor_tensor(tail[:], xf_sb[last][:].indirect(entries), spread[last][:, cols], ADD)
+            scale_into(last, q, tail[:])
 
         def multiply(q):
             nc.vector.quantize_mx(out=xs_codes[q][:].bitcast(FP8X4), scales=xs_scale[q][:], in_=xs[q][:])
@@ -156,7 +160,10 @@ def tile_list_member_plus_picked_group_pl_kernel(
 
         def drain(q):
             cols = slice(q * PIECE, (q + 1) * PIECE)
-            nc.scalar.copy(out=y[q][:], in_=acc[q][:])
+            if q == 2:
+                nc.vector.tensor_copy(out=y[q][:], in_=acc[q][:])
+            else:
+                nc.scalar.copy(out=y[q][:], in_=acc[q][:])
             nc.sync.dma_start(out=out_rows[:, :, cols], in_=y[q][:])
 
         def round_y(q):
@@ -172,8 +179,14 @@ def tile_list_member_plus_picked_group_pl_kernel(
                 both = slice((q - 1) * PIECE, (q + 1) * PIECE)
                 nc.sync.dma_start(out=out_words[:, both], in_=y_codes[:, both])
 
-        for step in range(PIECES + 4):
-            for lag, stage in ((0, gather_last), (1, multiply), (2, drain), (3, round_y), (4, hand_on)):
+        for q in range(PIECES - 1):
+            gather_last(q)
+        multiply(0)
+        gather_last(PIECES - 1)
+        for q in range(1, PIECES):
+            multiply(q)
+        for step in range(PIECES + 2):
+            for lag, stage in ((0, drain), (1, round_y), (2, hand_on)):
                 if 0 <= step - lag < PIECES:
                     stage(step - lag)
 

from contextlib import ExitStack

import concourse.mybir as mybir

K, T, J, L, N, B, S = 512, 2048, 512, 512, 512, 64, 512
FLOPS = 2 * K * N * J + 2 * L * N * J

F32 = mybir.dt.float32
BF16 = mybir.dt.bfloat16
I32 = mybir.dt.int32
U16 = mybir.dt.uint16
U8 = mybir.dt.uint8
FP8X4 = mybir.dt.float8_e4m3fn_x4
FP4X4 = mybir.dt.float4_e2m1fn_x4
ADD = mybir.AluOpType.add
MULT = mybir.AluOpType.mult
COPY = mybir.ActivationFunctionType.Copy

P = 128
PACK = 4
GROUP = J // B
PIECE = 128
PIECES = J // PIECE


def load_scale_rows(queue, plane, scales, quads):
    for quad in quads:
        queue.dma_start(
            out=plane[32 * quad : 32 * quad + 4, :].bitcast(I32),
            in_=scales[0, 4 * quad : 4 * quad + 4, :].bitcast(I32),
        )


def tile_list_member_plus_picked_group_pl_kernel(
    tc, xf, gv, fk, w_words, w_scales, sx_words, sx_scales, ws_words, ws_scales, offs, offs2, out_0, out_1, out_2
):
    nc = tc.nc
    with ExitStack() as ctx:
        sb = ctx.enter_context(tc.tile_pool(name="sb", bufs=1))
        psum = ctx.enter_context(tc.psum_pool(name="psum", bufs=1))

        slot_list = sb.tile([P, J // 16], U16, name="slot_list")
        group_list = sb.tile([P, B // 16], U16, name="group_list")
        gv_sb = sb.tile([P, PACK * S], F32, name="gv_sb")
        fk_sb = sb.tile([P, PACK], F32, name="fk_sb")
        xf_sb = [sb.tile([P, T], F32, name="xf_sb%d" % t) for t in range(PACK)]
        w_raw = sb.tile([P, N], I32, name="w_raw")
        ws_raw = sb.tile([P, N], I32, name="ws_raw")
        w_scale_raw = sb.tile([P, N], U8, name="w_scale_raw")
        ws_scale_raw = sb.tile([P, N], U8, name="ws_scale_raw")
        sx_codes = sb.tile([P, 2 * J], U8, name="sx_codes", align_bytes=64)
        sx_scale = sb.tile([P, J], U8, name="sx_scale", align_bytes=64)

        for plane in (ws_scale_raw, w_scale_raw, sx_scale):
            nc.vector.memset(plane[:].bitcast(I32), 0)

        xf_planes = xf.rearrange("(p t) c -> p t c", t=PACK)
        nc.sync.dma_start(out=gv_sb[:], in_=gv.rearrange("(p t) s -> p (t s)", t=PACK))
        nc.sync.dma_start(group_list[:], offs2)
        nc.sync.dma_start(slot_list[:], offs)
        nc.sync.dma_start(out=fk_sb[:], in_=fk.rearrange("(p t) o -> p (t o)", t=PACK))
        nc.sync.dma_start(out=xf_sb[0][:], in_=xf_planes[:, 0, :])
        load_scale_rows(nc.sync, ws_scale_raw, ws_scales, range(4))
        load_scale_rows(nc.sync, w_scale_raw, w_scales, range(2))
        nc.sync.dma_start(out=xf_sb[1][:], in_=xf_planes[:, 1, :])
        load_scale_rows(nc.sync, w_scale_raw, w_scales, range(2, 4))
        load_scale_rows(nc.sync, sx_scale, sx_scales, range(4))
        nc.sync.dma_start(out=xf_sb[2][:], in_=xf_planes[:, 2, :])
        nc.sync.dma_start(out=ws_raw[:], in_=ws_words[0].rearrange("p n t -> p (n t)").bitcast(I32))
        nc.sync.dma_start(out=sx_codes[:].bitcast(I32), in_=sx_words[0].bitcast(I32))
        nc.sync.dma_start(out=w_raw[:], in_=w_words[0].rearrange("p n t -> p (n t)").bitcast(I32))
        nc.sync.dma_start(out=xf_sb[3][:], in_=xf_planes[:, 3, :])

        picked = sb.tile([P, PACK, B], F32, name="picked")
        spread = [sb.tile([P, J], F32, name="spread%d" % t) for t in range(PACK)]
        for t in range(PACK):
            nc.vector.tensor_copy(picked[:, t, :], gv_sb[:, t * S : (t + 1) * S].indirect(group_list[:]))
        for t in range(PACK):
            nc.vector.tensor_copy(
                spread[t][:].rearrange("p (b e) -> p b e", e=GROUP),
                picked[:, t, :].unsqueeze(2).to_broadcast([P, B, GROUP]),
            )

        xs = [sb.tile([P, PIECE * PACK], BF16, name="xs%d" % q, tag="xs%d" % q, align_bytes=64) for q in range(PIECES)]
        summed = [sb.tile([P, J], F32, name="summed%d" % t) for t in range(PACK - 1)]

        def scale_into(t, q, src):
            dst = xs[q][:].rearrange("p (j t) -> p j t", t=PACK)[:, :, t]
            if q == PIECES - 1 and t >= 2:
                nc.vector.tensor_scalar(dst, src, fk_sb[:, t : t + 1], None, MULT)
            else:
                nc.scalar.activation(out=dst, in_=src, func=COPY, scale=fk_sb[:, t : t + 1])

        def deal(dst, src, run):
            nc.vector.tensor_copy(
                dst[:].rearrange("p (t c i) -> p c t i", t=PACK, i=run),
                src[:].rearrange("p (c i t) -> p c t i", t=PACK, i=run),
            )

        w_codes = sb.tile([P, N], I32, name="w_codes", align_bytes=64)
        ws_codes = sb.tile([P, N], I32, name="ws_codes", align_bytes=64)
        w_scale = sb.tile([P, N], U8, name="w_scale", align_bytes=64)
        ws_scale = sb.tile([P, N], U8, name="ws_scale", align_bytes=64)

        for t in range(PACK - 1):
            nc.vector.tensor_tensor(summed[t][:], xf_sb[t][:].indirect(slot_list[:]), spread[t][:], ADD)
            for q in range(PIECES):
                scale_into(t, q, summed[t][:, q * PIECE : (q + 1) * PIECE])
            if t == 0:
                deal(ws_scale, ws_scale_raw, 16)
            if t == 1:
                deal(w_scale, w_scale_raw, 16)
            if t == 2:
                deal(ws_codes, ws_raw, 4)
                deal(w_codes, w_raw, 4)

        acc = [psum.tile([P, PACK, PIECE], F32, name="acc%d" % q) for q in range(PIECES)]
        for q in range(PIECES):
            for t in range(PACK):
                nc.tensor.matmul_mx(
                    out=acc[q][:, t, :],
                    lhsT=ws_codes[:, t * P : (t + 1) * P].bitcast(FP8X4),
                    lhsT_scale=ws_scale[:, t * P : (t + 1) * P],
                    rhs=sx_codes[:, 2 * q * PIECE : 2 * (q + 1) * PIECE].bitcast(FP4X4),
                    rhs_scale=sx_scale[:, q * PIECE : (q + 1) * PIECE],
                    start=(t == 0),
                    stop=False,
                )

        xs_codes = [sb.tile([P, PIECE], I32, name="xs_codes%d" % q, align_bytes=64) for q in range(PIECES)]
        xs_scale = [sb.tile([P, PIECE], U8, name="xs_scale%d" % q, align_bytes=64) for q in range(PIECES)]
        y = [sb.tile([P, PACK, PIECE], F32, name="y%d" % q) for q in range(PIECES)]
        y_round = [sb.tile([P, PIECE * PACK], BF16, name="y_round%d" % q, align_bytes=64) for q in range(PIECES)]
        y_codes = sb.tile([P, J], I32, name="y_codes", align_bytes=64)
        y_scale = sb.tile([P, J], U8, name="y_scale", align_bytes=64)
        out_rows = out_0.rearrange("(p t) j -> p t j", t=PACK)
        out_words = out_1[0].rearrange("p c t -> p (c t)").bitcast(I32)
        last = PACK - 1

        def gather_last(q):
            cols = slice(q * PIECE, (q + 1) * PIECE)
            entries = slot_list[:, q * PIECE // 16 : (q + 1) * PIECE // 16]
            tag = "xs0" if q == PIECES - 1 else "tail%d" % q
            tail = sb.tile([P, PIECE], F32, name="tail%d" % q, tag=tag, align_bytes=64)
            nc.vector.tensor_tensor(tail[:], xf_sb[last][:].indirect(entries), spread[last][:, cols], ADD)
            scale_into(last, q, tail[:])

        def multiply(q):
            nc.vector.quantize_mx(out=xs_codes[q][:].bitcast(FP8X4), scales=xs_scale[q][:], in_=xs[q][:])
            for t in range(PACK):
                nc.tensor.matmul_mx(
                    out=acc[q][:, t, :],
                    lhsT=w_codes[:, t * P : (t + 1) * P].bitcast(FP8X4),
                    lhsT_scale=w_scale[:, t * P : (t + 1) * P],
                    rhs=xs_codes[q][:].bitcast(FP8X4),
                    rhs_scale=xs_scale[q][:],
                    start=False,
                    stop=(t == PACK - 1),
                )

        def drain(q):
            cols = slice(q * PIECE, (q + 1) * PIECE)
            if q == 2:
                nc.vector.tensor_copy(out=y[q][:], in_=acc[q][:])
            else:
                nc.scalar.copy(out=y[q][:], in_=acc[q][:])
            nc.sync.dma_start(out=out_rows[:, :, cols], in_=y[q][:])

        def round_y(q):
            nc.vector.tensor_copy(
                y_round[q][:].rearrange("p (c i t) -> p c t i", t=PACK, i=4),
                y[q][:].rearrange("p t (c i) -> p c t i", i=4),
            )

        def hand_on(q):
            cols = slice(q * PIECE, (q + 1) * PIECE)
            nc.vector.quantize_mx(out=y_codes[:, cols].bitcast(FP8X4), scales=y_scale[:, cols], in_=y_round[q][:])
            if q % 2 == 1:
                both = slice((q - 1) * PIECE, (q + 1) * PIECE)
                nc.sync.dma_start(out=out_words[:, both], in_=y_codes[:, both])

        for q in range(PIECES - 1):
            gather_last(q)
        multiply(0)
        gather_last(PIECES - 1)
        for q in range(1, PIECES):
            multiply(q)
        for step in range(PIECES + 2):
            for lag, stage in ((0, drain), (1, round_y), (2, hand_on)):
                if 0 <= step - lag < PIECES:
                    stage(step - lag)

        for quad in range(4):
            queue = nc.sync if quad % 2 == 0 else nc.scalar
            queue.dma_start(
                out=out_2[0, 4 * quad : 4 * quad + 4, :].bitcast(I32),
                in_=y_scale[32 * quad : 32 * quad + 4, :].bitcast(I32),
            )
